import numpy as np
import ml_dtypes


def mxq(x, axis, fmt="e4m3"):
    dtype, down = {"e4m3": (ml_dtypes.float8_e4m3fn, 7), "e5m2": (ml_dtypes.float8_e5m2, 14)}[fmt]
    v = np.moveaxis(np.asarray(x, np.float32).astype(ml_dtypes.bfloat16).astype(np.float64), axis, -1)
    blocks = v.reshape(v.shape[:-1] + (-1, 32))
    amax = np.abs(blocks).max(-1, keepdims=True)
    byte = np.maximum(np.where(amax > 0, np.frexp(amax)[1] - 1 + 127, 0) - down, 1)
    scale = np.exp2(byte - 127.0)
    codes = (blocks / scale).astype(np.float32).astype(dtype).astype(np.float64)
    return np.moveaxis((codes * scale).reshape(v.shape), -1, axis)


WIDE = False


def mx_kscale(k):
    if not WIDE:
        return np.ones(k)
    levels = np.array([10, -10, 5, -5, 0])
    if k % 512:
        return np.exp2(np.random.permutation(np.resize(levels, k // 32))).repeat(32)
    a = np.empty((k // 512, 16))
    for p in range(k // 512):
        a[p, :8] = np.random.permutation(np.resize(levels, 8))
        for g in range(8):
            far = levels[np.abs(levels - a[p, g]) >= 10]
            a[p, g + 8] = far[np.random.randint(len(far))]
    return np.exp2(a.ravel()).repeat(32)


def f64(x):
    return np.asarray(x).astype(np.float64)


def striped(idx):
    return np.tile(idx.reshape(-1, 16).T, (8, 1)).astype(np.uint16)


def unstriped(offs):
    return offs[:16].T.reshape(-1).astype(np.int64)


def pack_weight(w):
    k, n = w.shape
    w = f64(np.asarray(w, np.float32).astype(ml_dtypes.bfloat16)).reshape(k // 32, 32, n)
    amax = np.abs(w).max(1)
    byte = np.clip(np.where(amax > 0, np.frexp(amax)[1] - 1 + 127 - 7, 1), 1, 254)
    scaled = (w * np.exp2(127.0 - byte)[:, None, :]).reshape(k, n).astype(np.float32)
    words = np.ascontiguousarray(scaled.reshape(k // 512, 128, 4, n).transpose(0, 1, 3, 2)).astype(ml_dtypes.float8_e4m3fn).view(np.uint8)
    return words, np.ascontiguousarray(byte.astype(np.uint8).reshape(k // 512, 16, n))


def unpack_weight(words, scales):
    g, p, n, _ = words.shape
    vals = np.ascontiguousarray(words).view(ml_dtypes.float8_e4m3fn).astype(np.float64) * np.repeat(np.exp2(scales.astype(np.float64) - 127.0), 8, axis=1)[..., None]
    return vals.transpose(0, 1, 3, 2).reshape(g * 512, n)


def sigmoid(v):
    return 1.0 / (1.0 + np.exp(-np.maximum(v, -700.0)))


K, T, S, J, H, N = 1024, 1024, 512, 512, 512, 128


def setup_inputs():
    n = np.random.standard_normal
    s = mx_kscale(K)[:, None]
    u = mx_kscale(H)
    r = mx_kscale(J)[:, None]
    packed = pack_weight(n((K, T)) * s)
    return {
        "x_words": packed[0],
        "x_scales": packed[1],
        "eT": (n((J, S)) * r).astype(np.float32),
        "w1": (n((K, H)) / np.sqrt(K) / s * u).astype(np.float32),
        "w3": (n((J, H)) / np.sqrt(J) / r).astype(np.float32),
        "w2": (n((H, N)) / np.sqrt(H) / u[:, None]).astype(np.float32),
        "offs": striped(np.random.permutation(T)[:S]),
    }


def reference(x_words, x_scales, eT, w1, w3, w2, offs):
    c = mxq(f64(w1), 0, "e4m3").T @ unpack_weight(x_words, x_scales)[:, unstriped(offs)]
    z = c * sigmoid(mxq(f64(w3), 0, "e4m3").T @ mxq(f64(eT), 0, "e4m3"))
    return mxq(f64(w2), 0, "e4m3").T @ mxq(z, 0, "e4m3")

from contextlib import ExitStack

import concourse.mybir as mybir

K, T, S, J, H, N = 1024, 1024, 512, 512, 512, 128
FLOPS = 2 * (K * H * S + J * H * S + H * N * S)

F32 = mybir.dt.float32
BF16 = mybir.dt.bfloat16
I32 = mybir.dt.int32
U32 = mybir.dt.uint32
U16 = mybir.dt.uint16
U8 = mybir.dt.uint8
FP8X4 = mybir.dt.float8_e4m3fn_x4
SIGMOID = mybir.ActivationFunctionType.Sigmoid
MULT = mybir.AluOpType.mult

P = 128
PACK = 4
K_PASS = P * PACK
CHUNK = 128
CHUNKS = S // CHUNK
LIST_COLS = CHUNK // 16
SCALAR_SHARE = 92
RAW = 0
STAGE = 8192


def tile_picked_schnet_sigmoid_p_kernel(tc, x_words, x_scales, eT, w1, w3, w2, offs, out):
    nc = tc.nc
    with ExitStack() as ctx:
        sb = ctx.enter_context(tc.tile_pool(name="sb", bufs=1))
        shared = ctx.enter_context(tc.tile_pool(name="shared", bufs=1))
        ps = ctx.enter_context(tc.psum_pool(name="ps", bufs=1))

        def place(shape, dtype, name, at):
            if at is None:
                return sb.tile(shape, dtype, name=name, align_bytes=64)
            return shared.tile(shape, dtype, name=name, align_bytes=64, offset=at)

        def mx_tiles(name, width, at=None):
            codes = place([P, width], U32, name + "_codes", at)
            scales = place([P, width], U8, name + "_scales", None if at is None else at + 4 * width)
            return codes, scales

        def quantize(operand, grouped):
            nc.vector.quantize_mx(out=operand[0][:].bitcast(FP8X4), scales=operand[1][:], in_=grouped)

        def load_weight(name, rows, at=None):
            raw = place([P, PACK, P, PACK], F32, name + "_raw", at)
            nc.sync.dma_start(out=raw[:].rearrange("p j m t -> p (j m t)"), in_=rows.rearrange("(p j) c -> p (j c)", j=PACK))
            return raw

        def load_plain(name, rows):
            raw = sb.tile([P, PACK, rows.shape[1]], F32, name=name + "_raw")
            nc.sync.dma_start(out=raw[:], in_=rows.rearrange("(p j) c -> p j c", j=PACK))
            return raw

        def load_words(o):
            words = sb.tile([P, T], U32, name="x_words%d" % o)
            nc.sync.dma_start(out=words[:].bitcast(I32), in_=x_words[o].rearrange("p c r -> p (c r)").bitcast(I32))
            return words

        def prepare_weight(name, raw):
            grouped = place([P, PACK, P, PACK], BF16, name + "_bf16", STAGE)
            src = raw[:].rearrange("p j m t -> p m j t")
            dst = grouped[:].rearrange("p t m j -> p m j t")
            nc.scalar.copy(out=dst[:, :SCALAR_SHARE, :, 2:], in_=src[:, :SCALAR_SHARE, :, 2:])
            nc.vector.tensor_copy(out=dst[:, :, :, :2], in_=src[:, :, :, :2])
            nc.vector.tensor_copy(out=dst[:, SCALAR_SHARE:, :, 2:], in_=src[:, SCALAR_SHARE:, :, 2:])
            halves = []
            for u in range(2):
                halves.append(mx_tiles("%s_%d" % (name, u), 2 * P))
                quantize(halves[u], grouped[:, 2 * u : 2 * u + 2].rearrange("p t m j -> p (t m j)"))
            return halves

        def round_plain(name, raw_cols, copy, at=None):
            grouped = place([P, CHUNK, PACK], BF16, name + "_bf16", at)
            copy(out=grouped[:].rearrange("p (c i) j -> p c j i", i=4), in_=raw_cols.rearrange("p j (c i) -> p c j i", i=4))
            return grouped

        def quantize_plain(name, grouped, at=None):
            operand = mx_tiles(name, CHUNK, at)
            quantize(operand, grouped[:].rearrange("p c j -> p (c j)"))
            return operand

        def matmul(dst, lhs, cols, rhs_codes, rhs_scales, start, stop):
            nc.tensor.matmul_mx(out=dst, lhsT=lhs[0][:, cols].bitcast(FP8X4), lhsT_scale=lhs[1][:, cols],
                                rhs=rhs_codes.bitcast(FP8X4), rhs_scale=rhs_scales, start=start, stop=stop)

        x_sc = sb.tile([P, T], U8, name="x_sc")
        nc.vector.memset(x_sc[:].bitcast(I32), 0)

        warm_in = sb.tile([P, 1], F32, name="warm_in")
        warm_out = sb.tile([P, 1], F32, name="warm_out")
        nc.vector.memset(warm_in[:], 0.0)
        nc.scalar.activation(out=warm_out[:], in_=warm_in[:], func=SIGMOID)

        words = [load_words(0)]
        offsets = sb.tile([P, S // 16], U16, name="offsets")
        nc.sync.dma_start(offsets[:], offs)
        for q in range(4):
            nc.sync.dma_start(out=x_sc[32 * q : 32 * q + 8, :].bitcast(I32), in_=x_scales[:, 4 * q : 4 * q + 4, :].bitcast(I32))
        words.append(load_words(1))
        w1_raw = [load_weight("w1_%d" % o, w1[o * K_PASS : (o + 1) * K_PASS, :]) for o in range(2)]
        w3_raw = load_weight("w3", w3, RAW)
        e_raw = [load_plain("e0", eT[:, : S // 2])]
        e_raw.append(load_plain("e1", eT[:, S // 2 :]))
        w2_raw = load_plain("w2", w2)

        f_banks = [ps.tile([P, PACK, CHUNK], F32, name="f%d" % i) for i in range(CHUNKS)]
        c_banks = [ps.tile([P, PACK, CHUNK], F32, name="c%d" % i, tag="c%d" % i) for i in range(CHUNKS)]

        def round_edges(n, copy, at=None):
            return round_plain("e%d" % n, e_raw[n // 2][:, :, (n % 2) * CHUNK : (n % 2 + 1) * CHUNK], copy, at)

        def filter_chunk(n, e_mx):
            bank = f_banks[n]
            for t in range(PACK):
                matmul(bank[:, t, :], w3_mx[t // 2], slice(t % 2 * P, (t % 2 + 1) * P), e_mx[0][:], e_mx[1][:], True, True)
            gate = sb.tile([P, CHUNK, PACK], F32, name="gate%d" % n)
            nc.scalar.activation(out=gate[:], in_=bank[:].rearrange("p t n -> p n t"), func=SIGMOID)
            return gate

        picked_sc = sb.tile([P, S], U8, name="picked_sc", align_bytes=64)
        nc.vector.tensor_copy(picked_sc[:], x_sc[:].indirect(offsets[:]))
        picked = []
        for o in range(2):
            picked.append(sb.tile([P, S], U32, name="picked%d" % o, align_bytes=64))
            nc.vector.tensor_copy(picked[o][:], words[o][:].indirect(offsets[:]))
        w1_mx = [prepare_weight("w1_%d" % o, w1_raw[o]) for o in range(2)]
        for n in range(CHUNKS):
            cols = slice(n * CHUNK, (n + 1) * CHUNK)
            for t in range(PACK):
                for o in range(2):
                    matmul(c_banks[n][:, t, :], w1_mx[o][t // 2], slice(t % 2 * P, (t % 2 + 1) * P), picked[o][:, cols], picked_sc[4 * o :, cols], o == 0, o == 1)
        w3_mx = prepare_weight("w3", w3_raw)

        def gate_chunk(n):
            z = sb.tile([P, CHUNK, PACK], BF16, name="z%d" % n, align_bytes=64)
            nc.vector.tensor_tensor(z[:], c_banks[n][:].rearrange("p t n -> p n t"), gates[n][:], MULT)
            return z

        def project_chunk(n, z_mx):
            bank = ps.tile([P, CHUNK], F32, name="o%d" % n, tag="c%d" % n)
            matmul(bank[:], w2_mx, slice(0, N), z_mx[0][:], z_mx[1][:], True, True)
            res = sb.tile([P, CHUNK], F32, name="res%d" % n)
            nc.scalar.copy(out=res[:], in_=bank[:])
            nc.sync.dma_start(out=out[:, n * CHUNK : (n + 1) * CHUNK], in_=res[:])

        e_bf = [round_edges(n, nc.scalar.copy, RAW + 1024 * n) for n in range(2)]
        e_mx = [quantize_plain("e0", e_bf[0])]
        e_bf += [round_edges(2, nc.vector.tensor_copy, RAW + 2048), round_edges(3, nc.scalar.copy, RAW + 3072)]
        e_mx += [quantize_plain("e%d" % n, e_bf[n]) for n in (1, 2)]
        w2_bf = round_plain("w2", w2_raw[:], nc.vector.tensor_copy, RAW + 4096)
        e_mx.append(quantize_plain("e3", e_bf[3]))
        gates = [filter_chunk(n, e_mx[n]) for n in range(CHUNKS)]
        z = [gate_chunk(0)]
        w2_mx = quantize_plain("w2", w2_bf)
        for n in range(CHUNKS):
            if n + 1 < CHUNKS:
                z.append(gate_chunk(n + 1))
            project_chunk(n, quantize_plain("z%d" % n, z[n]))
